import numpy as np
import ml_dtypes


def mxq(x, axis, fmt="e4m3"):
    dtype, down = {"e4m3": (ml_dtypes.float8_e4m3fn, 7), "e5m2": (ml_dtypes.float8_e5m2, 14)}[fmt]
    v = np.moveaxis(np.asarray(x, np.float32).astype(ml_dtypes.bfloat16).astype(np.float64), axis, -1)
    blocks = v.reshape(v.shape[:-1] + (-1, 32))
    amax = np.abs(blocks).max(-1, keepdims=True)
    byte = np.maximum(np.where(amax > 0, np.frexp(amax)[1] - 1 + 127, 0) - down, 1)
    scale = np.exp2(byte - 127.0)
    codes = (blocks / scale).astype(np.float32).astype(dtype).astype(np.float64)
    return np.moveaxis((codes * scale).reshape(v.shape), -1, axis)


WIDE = False


def mx_kscale(k):
    if not WIDE:
        return np.ones(k)
    levels = np.array([10, -10, 5, -5, 0])
    if k % 512:
        return np.exp2(np.random.permutation(np.resize(levels, k // 32))).repeat(32)
    a = np.empty((k // 512, 16))
    for p in range(k // 512):
        a[p, :8] = np.random.permutation(np.resize(levels, 8))
        for g in range(8):
            far = levels[np.abs(levels - a[p, g]) >= 10]
            a[p, g + 8] = far[np.random.randint(len(far))]
    return np.exp2(a.ravel()).repeat(32)


def f64(x):
    return np.asarray(x).astype(np.float64)


def striped(idx):
    return np.tile(idx.reshape(-1, 16).T, (8, 1)).astype(np.uint16)


def unstriped(offs):
    return offs[:16].T.reshape(-1).astype(np.int64)


E2M1 = np.array([0.0, 0.5, 1.0, 1.5, 2.0, 3.0, 4.0, 6.0, -0.0, -0.5, -1.0, -1.5, -2.0, -3.0, -4.0, -6.0])


def pack_weight(w, fmt):
    k, n = w.shape
    w = f64(np.asarray(w, np.float32).astype(ml_dtypes.bfloat16)).reshape(k // 32, 32, n)
    amax = np.abs(w).max(1)
    if fmt == "e4m3":
        byte = np.frexp(amax)[1] - 1 + 127 - 7
    else:
        mant, ex = np.frexp(amax / 6.0)
        byte = np.where(mant > 0.5, ex, ex - 1) + 127
    byte = np.clip(np.where(amax > 0, byte, 1), 1, 254)
    scaled = (w * np.exp2(127.0 - byte)[:, None, :]).reshape(k, n).astype(np.float32)
    by_word = np.ascontiguousarray(scaled.reshape(k // 512, 128, 4, n).transpose(0, 1, 3, 2))
    if fmt == "e4m3":
        words = by_word.astype(ml_dtypes.float8_e4m3fn).view(np.uint8)
    else:
        c = by_word.astype(ml_dtypes.float4_e2m1fn).view(np.uint8) & 0xF
        words = (c[..., 0::2] | (c[..., 1::2] << 4)).reshape(k // 512, 128, 2 * n)
    return np.ascontiguousarray(words), np.ascontiguousarray(byte.astype(np.uint8).reshape(k // 512, 16, n))


def unpack_weight(words, scales, fmt):
    g, _, n = scales.shape
    words = np.ascontiguousarray(words).reshape(g, 128, n, -1)
    if fmt == "e4m3":
        vals = words.view(ml_dtypes.float8_e4m3fn).astype(np.float64)
    else:
        nib = np.empty((g, 128, n, 4), np.uint8)
        nib[..., 0::2] = words & 0xF
        nib[..., 1::2] = words >> 4
        vals = E2M1[nib]
    vals = vals * np.repeat(np.exp2(scales.astype(np.float64) - 127.0), 8, axis=1)[..., None]
    return vals.transpose(0, 1, 3, 2).reshape(g * 512, n)


def gelu(v):
    return 0.5 * v * (1.0 + np.tanh(np.sqrt(2.0 / np.pi) * (v + 0.044715 * v**3)))


K, K1, T, S, H, T3, S2, P = 1536, 512, 4096, 1024, 1024, 2048, 512, 512

def setup_inputs():
    n = np.random.standard_normal
    s = mx_kscale(K)[:, None]
    u = mx_kscale(H)[:, None]
    tab_words, tab_scales = pack_weight(n((K, T)) * s, "e4m3")
    tab2_words, tab2_scales = pack_weight(n((H, T3)) / np.sqrt(H) / u, "e4m3")
    w4_words, w4_scales = pack_weight(n((K1, H)) / np.sqrt(K) / s[:K1], "e2m1")
    return {
        "tab_words": tab_words, "tab_scales": tab_scales,
        "offs": striped(np.random.permutation(T)[:S]),
        "tab2_words": tab2_words, "tab2_scales": tab2_scales,
        "offs2": striped(np.random.permutation(T3)[:S2]),
        "pos1": striped(np.random.permutation(S)[:P]),
        "pos2": striped(np.random.permutation(S)[:P]),
        "w4_words": w4_words, "w4_scales": w4_scales,
        "w1": (n((K - K1, H)) / np.sqrt(K) / s[K1:]).astype(np.float32),
        "freq": (np.random.uniform(0.42, 0.54, H) * np.sign(n(H))).astype(np.float32),
        "gain": (2.0 * np.exp(0.3 * n(H)) * u[:, 0]).astype(np.float32),
        "wish": (0.5 * n((H, P)) * u).astype(np.float32),
        "tent": np.exp(0.4 * n(H)).astype(np.float32),
        "occ": (0.5 * n((S2, P))).astype(np.float32),
    }

def reference(tab_words, tab_scales, offs, tab2_words, tab2_scales, offs2, pos1, pos2,
              w4_words, w4_scales, w1, freq, gain, wish, tent, occ):
    v = unpack_weight(tab_words, tab_scales, "e4m3")[:, unstriped(offs)]
    v2 = unpack_weight(tab2_words, tab2_scales, "e4m3")[:, unstriped(offs2)]
    w4 = unpack_weight(w4_words, w4_scales, "e2m1")
    d = w4.T @ v[:K1] + mxq(f64(w1), 0, "e4m3").T @ v[K1:]
    h = f64(gain)[:, None] * np.sin(f64(freq)[:, None] * d)
    x1 = h[:, unstriped(pos1)] + f64(wish)
    x2 = f64(tent)[:, None] * h[:, unstriped(pos2)]
    e1 = v2.T @ mxq(x1, 0, "e4m3")
    e2 = v2.T @ mxq(x2, 0, "e4m3")
    return np.maximum(e1, e2) + f64(occ)

@@ -1,0 +1,277 @@
+from contextlib import ExitStack
+
+import concourse.mybir as mybir
+
+K, K1, T, S, H, T3, S2, NP = 1536, 512, 4096, 1024, 1024, 2048, 512, 512
+FLOPS = 2 * K * H * S + 2 * 2 * H * S2 * NP
+
+F32 = mybir.dt.float32
+BF16 = mybir.dt.bfloat16
+I32 = mybir.dt.int32
+U32 = mybir.dt.uint32
+U16 = mybir.dt.uint16
+U8 = mybir.dt.uint8
+FP8X4 = mybir.dt.float8_e4m3fn_x4
+FP4X4 = mybir.dt.float4_e2m1fn_x4
+ACT = mybir.ActivationFunctionType
+ALU = mybir.AluOpType
+
+P = 128
+PACK = 4
+PASS = P * PACK
+BANK = 512
+HALF = NP // 2
+
+
+def tile_list_pitch_proposal_scores_kernel(
+    tc, tab_words, tab_scales, offs, tab2_words, tab2_scales, offs2, pos1, pos2,
+    w4_words, w4_scales, w1, freq, gain, wish, tent, occ, out,
+):
+    nc = tc.nc
+    with ExitStack() as ctx:
+        lists = ctx.enter_context(tc.tile_pool(name="lists", bufs=1))
+        keep = ctx.enter_context(tc.tile_pool(name="keep", bufs=1))
+        ring = ctx.enter_context(tc.tile_pool(name="ring", bufs=1))
+        psum = ctx.enter_context(tc.psum_pool(name="psum", bufs=1))
+
+        offs_t = lists.tile([P, S // 16], U16, name="offs_t")
+        offs2_t = lists.tile([P, S2 // 16], U16, name="offs2_t")
+        pos1_t = lists.tile([P, NP // 16], U16, name="pos1_t")
+        pos2_t = lists.tile([P, NP // 16], U16, name="pos2_t")
+
+        tab_sc = keep.tile([P, T], U8, name="tab_sc")
+        w4_sc_raw = keep.tile([P, H], U8, name="w4_sc_raw")
+        tab2_sc = keep.tile([P, T3], U8, name="tab2_sc")
+        for t in (tab_sc, w4_sc_raw, tab2_sc):
+            nc.vector.memset(t[:].bitcast(I32), 0)
+
+        freq_t = keep.tile([P, 2, PACK], F32, name="freq_t")
+        gain_t = keep.tile([P, 2, PACK], F32, name="gain_t")
+        tent_t = keep.tile([P, 2, PACK], F32, name="tent_t")
+
+        def load_words(words, a, width, name):
+            t = ring.tile([P, width], I32, name=name, tag="table", bufs=3)
+            nc.sync.dma_start(t[:], words[a].rearrange("p t i -> p (t i)").bitcast(I32))
+            return t
+
+        def load_w1(a, c0, width, name):
+            t = keep.tile([P, PACK, width], F32, name=name)
+            rows = w1[PASS * a : PASS * (a + 1), c0 : c0 + width]
+            nc.sync.dma_start(t[:], rows.rearrange("(p j) c -> p j c", j=PACK))
+            return t
+
+        def load_wish(b):
+            t = keep.tile([P, PACK, NP], F32, name="wish%d" % b)
+            nc.sync.dma_start(t[:], wish[PASS * b : PASS * (b + 1), :].rearrange("(p i) j -> p i j", i=PACK))
+            return t
+
+        def load_rows(t, vec):
+            nc.sync.dma_start(t[:], vec.rearrange("(b p i) -> p b i", b=2, i=PACK))
+
+        def load_scales(t, scales):
+            rows = 4 * scales.shape[0]
+            for q in range(4):
+                nc.sync.dma_start(t[32 * q : 32 * q + rows, :].bitcast(I32), scales[:, 4 * q : 4 * q + 4, :].bitcast(I32))
+
+        nc.sync.dma_start(offs_t[:], offs)
+        tab_w = [load_words(tab_words, 0, T, "tab0")]
+        load_scales(tab_sc, tab_scales)
+        w4_raw = keep.tile([P, H // 2], I32, name="w4_raw")
+        nc.sync.dma_start(w4_raw[:], w4_words[0].bitcast(I32))
+        tab_w.append(load_words(tab_words, 1, T, "tab1"))
+        load_scales(w4_sc_raw, w4_scales)
+        load_rows(tent_t, tent)
+        w1_00 = load_w1(0, 0, PASS, "w1_00")
+        tab_w.append(load_words(tab_words, 2, T, "tab2nd"))
+        load_rows(freq_t, freq)
+        load_rows(gain_t, gain)
+        nc.sync.dma_start(pos2_t[:], pos2)
+        w1_10 = [load_w1(1, 0, PASS // 2, "w1_10a"), load_w1(1, PASS // 2, PASS // 2, "w1_10b")]
+        w1_01 = load_w1(0, PASS, PASS, "w1_01")
+        nc.sync.dma_start(pos1_t[:], pos1)
+        w1_11 = load_w1(1, PASS, PASS, "w1_11")
+        wish_t = [load_wish(0), load_wish(1)]
+        load_scales(tab2_sc, tab2_scales)
+        nc.sync.dma_start(offs2_t[:], offs2)
+        tab2_w = [load_words(tab2_words, a, T3, "cand%d" % a) for a in range(2)]
+        occ_t = ring.tile([P, 4, NP], F32, name="occ_t", tag="table", bufs=3)
+        nc.sync.dma_start(occ_t[:], occ.rearrange("(t p) j -> p t j", p=P))
+
+        tent_wide = [keep.tile([P, PACK, w], F32, name="tent_wide%d" % b) for b, w in enumerate((NP, HALF))]
+        for b in range(2):
+            nc.scalar.copy(tent_wide[b][:], tent_t[:, b, :].unsqueeze(2).to_broadcast(list(tent_wide[b].shape)))
+
+        v_w = [keep.tile([P, S], U32, name="v_w%d" % a, align_bytes=64) for a in range(3)]
+        v_sc = keep.tile([P, S], U8, name="v_sc", align_bytes=64)
+        nc.vector.tensor_copy(v_w[0][:], tab_w[0][:].bitcast(U32).indirect(offs_t[:]))
+        nc.vector.tensor_copy(v_sc[:], tab_sc[:].indirect(offs_t[:]))
+
+        w4_c = keep.tile([P, 2 * H], U8, name="w4_c", align_bytes=64)
+        w4_sc = keep.tile([P, H], U8, name="w4_sc", align_bytes=64)
+        nc.vector.tensor_copy(
+            w4_c[:].bitcast(U16).rearrange("p (b i q) -> p b i q", b=2, i=PACK),
+            w4_raw[:].bitcast(U16).rearrange("p (b q i) -> p b i q", b=2, i=PACK),
+        )
+        nc.vector.tensor_copy(
+            w4_sc[:].rearrange("p (b i q) -> p b i q", b=2, i=PACK),
+            w4_sc_raw[:].rearrange("p (b q i) -> p b i q", b=2, i=PACK),
+        )
+
+        nc.vector.tensor_copy(v_w[1][:], tab_w[1][:].bitcast(U32).indirect(offs_t[:]))
+
+        def bf_tile(width, name):
+            return ring.tile([P, width], BF16, name=name, tag="rounded", bufs=3, align_bytes=64)
+
+        def deal_w1(copy, grouped, raw, q0):
+            nq = raw.shape[2] // PACK
+            dst = grouped[:].rearrange("p (i q j) -> p q j i", i=PACK, j=PACK)[:, q0 : q0 + nq]
+            copy(dst, raw[:].rearrange("p j (q i) -> p q j i", i=PACK))
+
+        def quantise(grouped, name, pieces=1):
+            width = grouped.shape[1] // PACK
+            codes = keep.tile([P, width], U32, name=name + "_c", align_bytes=64)
+            scales = keep.tile([P, width], U8, name=name + "_s", align_bytes=64)
+            step = width // pieces
+            for c in range(0, width, step):
+                nc.vector.quantize_mx(
+                    out=codes[:, c : c + step].bitcast(FP8X4),
+                    scales=scales[:, c : c + step],
+                    in_=grouped[:, PACK * c : PACK * (c + step)],
+                )
+            return codes, scales
+
+        def stage1_pass(banks, b, a, wq):
+            for i in range(PACK):
+                cols = slice(P * i, P * (i + 1))
+                if a == 0:
+                    c0 = PASS * b + P * i
+                    lhs = w4_c[:, 2 * c0 : 2 * (c0 + P)].bitcast(FP4X4)
+                    lhs_sc = w4_sc[:, c0 : c0 + P]
+                else:
+                    lhs = wq[0][:, cols].bitcast(FP8X4)
+                    lhs_sc = wq[1][:, cols]
+                for half in range(2):
+                    js = slice(BANK * half, BANK * (half + 1))
+                    nc.tensor.matmul_mx(
+                        out=banks[2 * i + half][:], lhsT=lhs, lhsT_scale=lhs_sc,
+                        rhs=v_w[a][:, js].bitcast(FP8X4), rhs_scale=v_sc[4 * a :, js],
+                        start=(a == 0), stop=(a == 2),
+                    )
+
+        def new_banks(name):
+            return [psum.tile([P, BANK], F32, name="%s%d" % (name, k), tag="bank%d" % k) for k in range(8)]
+
+        def sine(banks, b, i):
+            h = ring.tile([P, S], F32, name="h%d%d" % (b, i), tag="h", bufs=6)
+            for half in range(2):
+                nc.scalar.activation(
+                    h[:, BANK * half : BANK * (half + 1)], banks[2 * i + half][:], ACT.Sin, scale=freq_t[:, b, i : i + 1]
+                )
+            return h
+
+        def picked(width, name):
+            return ring.tile([P, PACK, width], F32, name=name, tag="picked", bufs=3)
+
+        def weave(src, name):
+            dst = bf_tile(PACK * src.shape[2], name)
+            nc.scalar.copy(
+                dst[:].rearrange("p (c k i) -> p c i k", k=4, i=PACK),
+                src[:].rearrange("p i (c k) -> p c i k", k=4),
+            )
+            return dst
+
+        banks = new_banks("d0_")
+        stage1_pass(banks, 0, 0, None)
+        g = bf_tile(PACK * PASS, "w1g_00")
+        deal_w1(nc.scalar.copy, g, w1_00, 0)
+        stage1_pass(banks, 0, 1, quantise(g, "w1q_00"))
+        nc.vector.tensor_copy(v_w[2][:], tab_w[2][:].bitcast(U32).indirect(offs_t[:]))
+        g = bf_tile(PACK * PASS, "w1g_10")
+        deal_w1(nc.scalar.copy, g, w1_10[0], 0)
+        deal_w1(nc.vector.tensor_copy, g, w1_10[1], P // 2)
+        stage1_pass(banks, 0, 2, quantise(g, "w1q_10", pieces=PACK))
+
+        h0 = []
+        x2_0 = picked(NP, "x2_0")
+        for i in range(PACK):
+            h = sine(banks, 0, i)
+            nc.vector.tensor_scalar(h[:], h[:], gain_t[:, 0, i : i + 1], None, ALU.mult)
+            nc.vector.tensor_tensor(x2_0[:, i, :], h[:].indirect(pos2_t[:]), tent_wide[0][:, i, :], ALU.mult)
+            h0.append(h)
+
+        banks = new_banks("d1_")
+        stage1_pass(banks, 1, 0, None)
+        for a, raw in ((1, w1_01), (2, w1_11)):
+            g = bf_tile(PACK * PASS, "w1g_%d1" % (a - 1))
+            deal_w1(nc.scalar.copy, g, raw, 0)
+            stage1_pass(banks, 1, a, quantise(g, "w1q_%d1" % (a - 1)))
+
+        x1_0 = picked(NP, "x1_0")
+        for i in range(PACK):
+            nc.vector.tensor_tensor(x1_0[:, i, :], h0[i][:].indirect(pos1_t[:]), wish_t[0][:, i, :], ALU.add)
+
+        h1 = []
+        x1_1 = picked(NP, "x1_1")
+        for i in range(PACK):
+            h = sine(banks, 1, i)
+            nc.scalar.activation(h[:], h[:], ACT.Copy, scale=gain_t[:, 1, i : i + 1])
+            nc.vector.tensor_tensor(x1_1[:, i, :], h[:].indirect(pos1_t[:]), wish_t[1][:, i, :], ALU.add)
+            h1.append(h)
+
+        c_w = [keep.tile([P, S2], U32, name="c_w%d" % a, align_bytes=64) for a in range(2)]
+        c_sc = keep.tile([P, S2], U8, name="c_sc", align_bytes=64)
+        for a in range(2):
+            nc.vector.tensor_copy(c_w[a][:], tab2_w[a][:].bitcast(U32).indirect(offs2_t[:]))
+        nc.vector.tensor_copy(c_sc[:], tab2_sc[:].indirect(offs2_t[:]))
+
+        x2q_0 = quantise(weave(x2_0, "x2g_0"), "x2q_0")
+        x1q_0 = quantise(weave(x1_0, "x1g_0"), "x1q_0")
+        x1g_1 = weave(x1_1, "x1g_1")
+
+        def stage2(dst, b, mt, xq, js, start, stop):
+            cols = slice(P * mt, P * (mt + 1))
+            nc.tensor.matmul_mx(
+                out=dst, lhsT=c_w[b][:, cols].bitcast(FP8X4), lhsT_scale=c_sc[4 * b :, cols],
+                rhs=xq[0][:, js].bitcast(FP8X4), rhs_scale=xq[1][:, js], start=start, stop=stop,
+            )
+
+        banks = new_banks("e_")
+        whole = slice(0, NP)
+        for mt in range(4):
+            stage2(banks[mt][:], 0, mt, x1q_0, whole, True, False)
+        for half in range(2):
+            for mt in range(4):
+                dst = banks[4 + 2 * half + mt // 2][:, HALF * (mt % 2) : HALF * (mt % 2 + 1)]
+                stage2(dst, 0, mt, x2q_0, slice(HALF * half, HALF * (half + 1)), mt % 2 == 0, False)
+
+        def pick_x2(half):
+            x = picked(HALF, "x2_1%d" % half)
+            for i in range(PACK):
+                nc.vector.tensor_tensor(
+                    x[:, i, :], h1[i][:].indirect(pos2_t[:, 16 * half : 16 * (half + 1)]), tent_wide[1][:, i, :], ALU.mult
+                )
+            return weave(x, "x2g_1%d" % half)
+
+        x2g = [pick_x2(0)]
+        x1q_1 = quantise(x1g_1, "x1q_1")
+        e1 = keep.tile([P, 4, NP], F32, name="e1")
+        for mt in range(4):
+            stage2(banks[mt][:], 1, mt, x1q_1, whole, False, True)
+        x2g.append(pick_x2(1))
+        for mt in range(4):
+            nc.scalar.copy(e1[:, mt, :], banks[mt][:])
+
+        out_v = out.rearrange("(t p) j -> p t j", p=P)
+        for half in range(2):
+            xq = quantise(x2g[half], "x2q_1%d" % half)
+            js = slice(HALF * half, HALF * (half + 1))
+            for mt in range(4):
+                dst = banks[4 + 2 * half + mt // 2][:, HALF * (mt % 2) : HALF * (mt % 2 + 1)]
+                stage2(dst, 1, mt, xq, slice(0, HALF), False, mt % 2 == 1)
+            res = [keep.tile([P, 2, HALF], F32, name="res%d%d" % (half, u)) for u in range(2)]
+            for u in range(2):
+                bank = banks[4 + 2 * half + u][:].rearrange("p (t j) -> p t j", t=2)
+                nc.vector.tensor_tensor(e1[:, 2 * u : 2 * u + 2, js], bank, e1[:, 2 * u : 2 * u + 2, js], ALU.max)
+            for u in range(2):
+                nc.vector.tensor_tensor(res[u][:], e1[:, 2 * u : 2 * u + 2, js], occ_t[:, 2 * u : 2 * u + 2, js], ALU.add)
+                nc.sync.dma_start(out_v[:, 2 * u : 2 * u + 2, js], res[u][:])

@@ -21,6 +21,7 @@ PACK = 4
 PASS = P * PACK
 BANK = 512
 HALF = NP // 2
+GAIN_ON_VECTOR = ((0, 0), (1, 3))
 
 
 def tile_list_pitch_proposal_scores_kernel(
@@ -54,8 +55,8 @@ def tile_list_pitch_proposal_scores_kernel(
             nc.sync.dma_start(t[:], words[a].rearrange("p t i -> p (t i)").bitcast(I32))
             return t
 
-        def load_w1(a, c0, width, name):
-            t = keep.tile([P, PACK, width], F32, name=name)
+        def load_w1(a, c0, width, name, tag):
+            t = ring.tile([P, PACK, width], F32, name=name, tag=tag)
             rows = w1[PASS * a : PASS * (a + 1), c0 : c0 + width]
             nc.sync.dma_start(t[:], rows.rearrange("(p j) c -> p j c", j=PACK))
             return t
@@ -71,33 +72,34 @@ def tile_list_pitch_proposal_scores_kernel(
         def load_scales(t, scales):
             rows = 4 * scales.shape[0]
             for q in range(4):
-                nc.sync.dma_start(t[32 * q : 32 * q + rows, :].bitcast(I32), scales[:, 4 * q : 4 * q + 4, :].bitcast(I32))
+                nc.gpsimd.dma_start(t[32 * q : 32 * q + rows, :].bitcast(I32), scales[:, 4 * q : 4 * q + 4, :].bitcast(I32))
 
+        load_scales(tab_sc, tab_scales)
+        load_scales(w4_sc_raw, w4_scales)
+        load_scales(tab2_sc, tab2_scales)
         nc.sync.dma_start(offs_t[:], offs)
         tab_w = [load_words(tab_words, 0, T, "tab0")]
-        load_scales(tab_sc, tab_scales)
+        load_rows(tent_t, tent)
         w4_raw = keep.tile([P, H // 2], I32, name="w4_raw")
         nc.sync.dma_start(w4_raw[:], w4_words[0].bitcast(I32))
         tab_w.append(load_words(tab_words, 1, T, "tab1"))
-        load_scales(w4_sc_raw, w4_scales)
-        load_rows(tent_t, tent)
-        w1_00 = load_w1(0, 0, PASS, "w1_00")
+        nc.sync.dma_start(offs2_t[:], offs2)
+        w1_00 = load_w1(0, 0, PASS, "w1_00", "slot_a")
         tab_w.append(load_words(tab_words, 2, T, "tab2nd"))
         load_rows(freq_t, freq)
         load_rows(gain_t, gain)
         nc.sync.dma_start(pos2_t[:], pos2)
-        w1_10 = [load_w1(1, 0, PASS // 2, "w1_10a"), load_w1(1, PASS // 2, PASS // 2, "w1_10b")]
-        w1_01 = load_w1(0, PASS, PASS, "w1_01")
         nc.sync.dma_start(pos1_t[:], pos1)
-        w1_11 = load_w1(1, PASS, PASS, "w1_11")
-        wish_t = [load_wish(0), load_wish(1)]
-        load_scales(tab2_sc, tab2_scales)
-        nc.sync.dma_start(offs2_t[:], offs2)
+        w1_10 = [load_w1(1, 0, PASS // 2, "w1_10a", "w1_10a"), load_w1(1, PASS // 2, PASS // 2, "w1_10b", "w1_10b")]
+        w1_01 = load_w1(0, PASS, PASS, "w1_01", "slot_b")
+        wish_t = [load_wish(0)]
+        w1_11 = load_w1(1, PASS, PASS, "w1_11", "w1_11")
+        wish_t.append(load_wish(1))
         tab2_w = [load_words(tab2_words, a, T3, "cand%d" % a) for a in range(2)]
         occ_t = ring.tile([P, 4, NP], F32, name="occ_t", tag="table", bufs=3)
         nc.sync.dma_start(occ_t[:], occ.rearrange("(t p) j -> p t j", p=P))
 
-        tent_wide = [keep.tile([P, PACK, w], F32, name="tent_wide%d" % b) for b, w in enumerate((NP, HALF))]
+        tent_wide = [keep.tile([P, PACK, w], F32, name="tent_wide%d" % b) for b, w in enumerate((NP, NP))]
         for b in range(2):
             nc.scalar.copy(tent_wide[b][:], tent_t[:, b, :].unsqueeze(2).to_broadcast(list(tent_wide[b].shape)))
 
@@ -162,116 +164,120 @@ def tile_list_pitch_proposal_scores_kernel(
             return [psum.tile([P, BANK], F32, name="%s%d" % (name, k), tag="bank%d" % k) for k in range(8)]
 
         def sine(banks, b, i):
-            h = ring.tile([P, S], F32, name="h%d%d" % (b, i), tag="h", bufs=6)
+            h = ring.tile([P, S], F32, name="h%d%d" % (b, i), tag="h", bufs=4)
             for half in range(2):
                 nc.scalar.activation(
                     h[:, BANK * half : BANK * (half + 1)], banks[2 * i + half][:], ACT.Sin, scale=freq_t[:, b, i : i + 1]
                 )
             return h
 
-        def picked(width, name):
-            return ring.tile([P, PACK, width], F32, name=name, tag="picked", bufs=3)
+        def picked(name, tag="picked", bufs=3):
+            return ring.tile([P, PACK, NP], F32, name=name, tag=tag, bufs=bufs)
 
-        def weave(src, name):
-            dst = bf_tile(PACK * src.shape[2], name)
-            nc.scalar.copy(
+        def weave(copy, src, dst):
+            copy(
                 dst[:].rearrange("p (c k i) -> p c i k", k=4, i=PACK),
-                src[:].rearrange("p i (c k) -> p c i k", k=4),
+                src.rearrange("p i (c k) -> p c i k", k=4),
             )
             return dst
 
-        banks = new_banks("d0_")
-        stage1_pass(banks, 0, 0, None)
+        def features(banks, b, i, x1, x2):
+            h = sine(banks, b, i)
+            if (b, i) in GAIN_ON_VECTOR:
+                nc.vector.tensor_scalar(h[:], h[:], gain_t[:, b, i : i + 1], None, ALU.mult)
+            else:
+                nc.scalar.activation(h[:], h[:], ACT.Copy, scale=gain_t[:, b, i : i + 1])
+            picks = [
+                (x2, pos2_t, tent_wide[b], ALU.mult),
+                (x1, pos1_t, wish_t[b], ALU.add),
+            ]
+            for x, pos, other, op in picks if b == 0 else reversed(picks):
+                nc.vector.tensor_tensor(x[:, i, :], h[:].indirect(pos[:]), other[:, i, :], op)
+
+        c_w = [keep.tile([P, S2], U32, name="c_w%d" % a, align_bytes=64) for a in range(2)]
+        c_sc = keep.tile([P, S2], U8, name="c_sc", align_bytes=64)
+        nc.vector.tensor_copy(c_sc[:], tab2_sc[:].indirect(offs2_t[:]))
+
+        banks0 = new_banks("d0_")
+        stage1_pass(banks0, 0, 0, None)
         g = bf_tile(PACK * PASS, "w1g_00")
         deal_w1(nc.scalar.copy, g, w1_00, 0)
-        stage1_pass(banks, 0, 1, quantise(g, "w1q_00"))
+        stage1_pass(banks0, 0, 1, quantise(g, "w1q_00"))
         nc.vector.tensor_copy(v_w[2][:], tab_w[2][:].bitcast(U32).indirect(offs_t[:]))
         g = bf_tile(PACK * PASS, "w1g_10")
         deal_w1(nc.scalar.copy, g, w1_10[0], 0)
         deal_w1(nc.vector.tensor_copy, g, w1_10[1], P // 2)
-        stage1_pass(banks, 0, 2, quantise(g, "w1q_10", pieces=PACK))
+        stage1_pass(banks0, 0, 2, quantise(g, "w1q_10", pieces=PACK))
+        g = bf_tile(PACK * PASS, "w1g_01")
+        deal_w1(nc.vector.tensor_copy, g, w1_01, 0)
+        w1q_01 = quantise(g, "w1q_01")
 
-        h0 = []
-        x2_0 = picked(NP, "x2_0")
-        for i in range(PACK):
-            h = sine(banks, 0, i)
-            nc.vector.tensor_scalar(h[:], h[:], gain_t[:, 0, i : i + 1], None, ALU.mult)
-            nc.vector.tensor_tensor(x2_0[:, i, :], h[:].indirect(pos2_t[:]), tent_wide[0][:, i, :], ALU.mult)
-            h0.append(h)
+        x2_0 = picked("x2_0", "slot_a", 1)
+        x1_0 = picked("x1_0")
+        for i in range(PACK - 1):
+            features(banks0, 0, i, x1_0, x2_0)
+        g = bf_tile(PACK * PASS, "w1g_11")
+        deal_w1(nc.scalar.copy, g, w1_11, 0)
+        w1q_11 = quantise(g, "w1q_11")
+        features(banks0, 0, PACK - 1, x1_0, x2_0)
 
-        banks = new_banks("d1_")
-        stage1_pass(banks, 1, 0, None)
-        for a, raw in ((1, w1_01), (2, w1_11)):
-            g = bf_tile(PACK * PASS, "w1g_%d1" % (a - 1))
-            deal_w1(nc.scalar.copy, g, raw, 0)
-            stage1_pass(banks, 1, a, quantise(g, "w1q_%d1" % (a - 1)))
-
-        x1_0 = picked(NP, "x1_0")
-        for i in range(PACK):
-            nc.vector.tensor_tensor(x1_0[:, i, :], h0[i][:].indirect(pos1_t[:]), wish_t[0][:, i, :], ALU.add)
-
-        h1 = []
-        x1_1 = picked(NP, "x1_1")
-        for i in range(PACK):
-            h = sine(banks, 1, i)
-            nc.scalar.activation(h[:], h[:], ACT.Copy, scale=gain_t[:, 1, i : i + 1])
-            nc.vector.tensor_tensor(x1_1[:, i, :], h[:].indirect(pos1_t[:]), wish_t[1][:, i, :], ALU.add)
-            h1.append(h)
-
-        c_w = [keep.tile([P, S2], U32, name="c_w%d" % a, align_bytes=64) for a in range(2)]
-        c_sc = keep.tile([P, S2], U8, name="c_sc", align_bytes=64)
+        banks1 = new_banks("d1_")
+        stage1_pass(banks1, 1, 0, None)
+        stage1_pass(banks1, 1, 1, w1q_01)
+        stage1_pass(banks1, 1, 2, w1q_11)
         for a in range(2):
             nc.vector.tensor_copy(c_w[a][:], tab2_w[a][:].bitcast(U32).indirect(offs2_t[:]))
-        nc.vector.tensor_copy(c_sc[:], tab2_sc[:].indirect(offs2_t[:]))
 
-        x2q_0 = quantise(weave(x2_0, "x2g_0"), "x2q_0")
-        x1q_0 = quantise(weave(x1_0, "x1g_0"), "x1q_0")
-        x1g_1 = weave(x1_1, "x1g_1")
-
-        def stage2(dst, b, mt, xq, js, start, stop):
-            cols = slice(P * mt, P * (mt + 1))
-            nc.tensor.matmul_mx(
-                out=dst, lhsT=c_w[b][:, cols].bitcast(FP8X4), lhsT_scale=c_sc[4 * b :, cols],
-                rhs=xq[0][:, js].bitcast(FP8X4), rhs_scale=xq[1][:, js], start=start, stop=stop,
-            )
+        x1_1 = picked("x1_1")
+        x2_1 = picked("x2_1")
+        features(banks1, 1, 0, x1_1, x2_1)
+        x2q_0 = quantise(weave(nc.scalar.copy, x2_0[:], bf_tile(PACK * NP, "x2g_0")), "x2q_0")
+        for i in range(1, PACK):
+            features(banks1, 1, i, x1_1, x2_1)
+        x1q_0 = quantise(weave(nc.scalar.copy, x1_0[:], bf_tile(PACK * NP, "x1g_0")), "x1q_0")
 
         banks = new_banks("e_")
-        whole = slice(0, NP)
-        for mt in range(4):
-            stage2(banks[mt][:], 0, mt, x1q_0, whole, True, False)
-        for half in range(2):
+
+        def stage2(side, half, b, xq, js):
             for mt in range(4):
-                dst = banks[4 + 2 * half + mt // 2][:, HALF * (mt % 2) : HALF * (mt % 2 + 1)]
-                stage2(dst, 0, mt, x2q_0, slice(HALF * half, HALF * (half + 1)), mt % 2 == 0, False)
-
-        def pick_x2(half):
-            x = picked(HALF, "x2_1%d" % half)
-            for i in range(PACK):
-                nc.vector.tensor_tensor(
-                    x[:, i, :], h1[i][:].indirect(pos2_t[:, 16 * half : 16 * (half + 1)]), tent_wide[1][:, i, :], ALU.mult
+                cols = slice(P * mt, P * (mt + 1))
+                nc.tensor.matmul_mx(
+                    out=banks[4 * side + 2 * half + mt // 2][:, HALF * (mt % 2) : HALF * (mt % 2 + 1)],
+                    lhsT=c_w[b][:, cols].bitcast(FP8X4), lhsT_scale=c_sc[4 * b :, cols],
+                    rhs=xq[0][:, js].bitcast(FP8X4), rhs_scale=xq[1][:, js],
+                    start=(b == 0 and mt % 2 == 0), stop=(b == 1 and mt % 2 == 1),
                 )
-            return weave(x, "x2g_1%d" % half)
 
-        x2g = [pick_x2(0)]
-        x1q_1 = quantise(x1g_1, "x1q_1")
-        e1 = keep.tile([P, 4, NP], F32, name="e1")
-        for mt in range(4):
-            stage2(banks[mt][:], 1, mt, x1q_1, whole, False, True)
-        x2g.append(pick_x2(1))
-        for mt in range(4):
-            nc.scalar.copy(e1[:, mt, :], banks[mt][:])
+        halves = [slice(HALF * half, HALF * (half + 1)) for half in range(2)]
+        for side, xq in ((0, x2q_0), (1, x1q_0)):
+            for half in range(2):
+                stage2(side, half, 0, xq, halves[half])
+
+        def half_tile(name):
+            return ring.tile([P, PACK * HALF], BF16, name=name, tag="half", bufs=4, align_bytes=64)
+
+        e1 = ring.tile([P, 4, NP], F32, name="e1", tag="slot_b")
+        x1g = [weave(nc.scalar.copy, x1_1[:, :, halves[half]], half_tile("x1g_1%d" % half)) for half in range(2)]
+        x2g = []
+        for half in range(2):
+            stage2(1, half, 1, quantise(x1g[half], "x1q_1%d" % half), halves[0])
+            x2g.append(weave(nc.vector.tensor_copy, x2_1[:, :, halves[half]], half_tile("x2g_1%d" % half)))
+            for u in range(2):
+                bank = banks[4 + 2 * half + u][:].rearrange("p (t j) -> p t j", t=2)
+                nc.scalar.copy(e1[:, 2 * u : 2 * u + 2, halves[half]], bank)
+        for half in range(2):
+            stage2(0, half, 1, quantise(x2g[half], "x2q_1%d" % half), halves[0])
 
         out_v = out.rearrange("(t p) j -> p t j", p=P)
         for half in range(2):
-            xq = quantise(x2g[half], "x2q_1%d" % half)
-            js = slice(HALF * half, HALF * (half + 1))
-            for mt in range(4):
-                dst = banks[4 + 2 * half + mt // 2][:, HALF * (mt % 2) : HALF * (mt % 2 + 1)]
-                stage2(dst, 1, mt, xq, slice(0, HALF), False, mt % 2 == 1)
-            res = [keep.tile([P, 2, HALF], F32, name="res%d%d" % (half, u)) for u in range(2)]
+            js = halves[half]
             for u in range(2):
-                bank = banks[4 + 2 * half + u][:].rearrange("p (t j) -> p t j", t=2)
+                bank = banks[2 * half + u][:].rearrange("p (t j) -> p t j", t=2)
                 nc.vector.tensor_tensor(e1[:, 2 * u : 2 * u + 2, js], bank, e1[:, 2 * u : 2 * u + 2, js], ALU.max)
+        for half in range(2):
+            js = halves[half]
+            adder = nc.gpsimd if half == 0 else nc.vector
             for u in range(2):
-                nc.vector.tensor_tensor(res[u][:], e1[:, 2 * u : 2 * u + 2, js], occ_t[:, 2 * u : 2 * u + 2, js], ALU.add)
-                nc.sync.dma_start(out_v[:, 2 * u : 2 * u + 2, js], res[u][:])
+                res = keep.tile([P, 2, HALF], F32, name="res%d%d" % (half, u))
+                adder.tensor_tensor(res[:], e1[:, 2 * u : 2 * u + 2, js], occ_t[:, 2 * u : 2 * u + 2, js], ALU.add)
+                nc.sync.dma_start(out_v[:, 2 * u : 2 * u + 2, js], res[:])

@@ -21,7 +21,6 @@ PACK = 4
 PASS = P * PACK
 BANK = 512
 HALF = NP // 2
-GAIN_ON_VECTOR = ((0, 0), (1, 3))
 
 
 def tile_list_pitch_proposal_scores_kernel(
@@ -94,8 +93,9 @@ def tile_list_pitch_proposal_scores_kernel(
         w1_01 = load_w1(0, PASS, PASS, "w1_01", "slot_b")
         wish_t = [load_wish(0)]
         w1_11 = load_w1(1, PASS, PASS, "w1_11", "w1_11")
+        tab2_w = [load_words(tab2_words, 0, T3, "cand0")]
         wish_t.append(load_wish(1))
-        tab2_w = [load_words(tab2_words, a, T3, "cand%d" % a) for a in range(2)]
+        tab2_w.append(load_words(tab2_words, 1, T3, "cand1"))
         occ_t = ring.tile([P, 4, NP], F32, name="occ_t", tag="table", bufs=3)
         nc.sync.dma_start(occ_t[:], occ.rearrange("(t p) j -> p t j", p=P))
 
@@ -163,14 +163,6 @@ def tile_list_pitch_proposal_scores_kernel(
         def new_banks(name):
             return [psum.tile([P, BANK], F32, name="%s%d" % (name, k), tag="bank%d" % k) for k in range(8)]
 
-        def sine(banks, b, i):
-            h = ring.tile([P, S], F32, name="h%d%d" % (b, i), tag="h", bufs=4)
-            for half in range(2):
-                nc.scalar.activation(
-                    h[:, BANK * half : BANK * (half + 1)], banks[2 * i + half][:], ACT.Sin, scale=freq_t[:, b, i : i + 1]
-                )
-            return h
-
         def picked(name, tag="picked", bufs=3):
             return ring.tile([P, PACK, NP], F32, name=name, tag=tag, bufs=bufs)
 
@@ -182,17 +174,24 @@ def tile_list_pitch_proposal_scores_kernel(
             return dst
 
         def features(banks, b, i, x1, x2):
-            h = sine(banks, b, i)
-            if (b, i) in GAIN_ON_VECTOR:
-                nc.vector.tensor_scalar(h[:], h[:], gain_t[:, b, i : i + 1], None, ALU.mult)
-            else:
+            h = ring.tile([P, S], F32, name="h%d%d" % (b, i), tag="h", bufs=4)
+            first = (b, i) == (0, 0)
+            for half in range(2):
+                js = slice(BANK * half, BANK * (half + 1))
+                nc.scalar.activation(h[:, js], banks[2 * i + half][:], ACT.Sin, scale=freq_t[:, b, i : i + 1])
+                if first:
+                    nc.scalar.activation(h[:, js], h[:, js], ACT.Copy, scale=gain_t[:, b, i : i + 1])
+            if not first:
                 nc.scalar.activation(h[:], h[:], ACT.Copy, scale=gain_t[:, b, i : i + 1])
             picks = [
                 (x2, pos2_t, tent_wide[b], ALU.mult),
                 (x1, pos1_t, wish_t[b], ALU.add),
             ]
-            for x, pos, other, op in picks if b == 0 else reversed(picks):
-                nc.vector.tensor_tensor(x[:, i, :], h[:].indirect(pos[:]), other[:, i, :], op)
+            width = HALF if (b, i) == (1, PACK - 1) else NP
+            for c in range(0, NP, width):
+                for x, pos, other, op in picks if b == 0 else reversed(picks):
+                    entries = pos[:, c // 16 : (c + width) // 16]
+                    nc.vector.tensor_tensor(x[:, i, c : c + width], h[:].indirect(entries), other[:, i, c : c + width], op)
 
         c_w = [keep.tile([P, S2], U32, name="c_w%d" % a, align_bytes=64) for a in range(2)]
         c_sc = keep.tile([P, S2], U8, name="c_sc", align_bytes=64)
@@ -257,16 +256,18 @@ def tile_list_pitch_proposal_scores_kernel(
             return ring.tile([P, PACK * HALF], BF16, name=name, tag="half", bufs=4, align_bytes=64)
 
         e1 = ring.tile([P, 4, NP], F32, name="e1", tag="slot_b")
-        x1g = [weave(nc.scalar.copy, x1_1[:, :, halves[half]], half_tile("x1g_1%d" % half)) for half in range(2)]
-        x2g = []
+        x1g = [weave(nc.scalar.copy, x1_1[:, :, halves[0]], half_tile("x1g_10"))]
+        x2g = [weave(nc.scalar.copy, x2_1[:, :, halves[0]], half_tile("x2g_10"))]
+        x1g.append(weave(nc.scalar.copy, x1_1[:, :, halves[1]], half_tile("x1g_11")))
+        stage2(1, 0, 1, quantise(x1g[0], "x1q_10"), halves[0])
+        x2g.append(weave(nc.vector.tensor_copy, x2_1[:, :, halves[1]], half_tile("x2g_11")))
+        stage2(0, 0, 1, quantise(x2g[0], "x2q_10"), halves[0])
+        stage2(1, 1, 1, quantise(x1g[1], "x1q_11"), halves[0])
+        stage2(0, 1, 1, quantise(x2g[1], "x2q_11"), halves[0])
         for half in range(2):
-            stage2(1, half, 1, quantise(x1g[half], "x1q_1%d" % half), halves[0])
-            x2g.append(weave(nc.vector.tensor_copy, x2_1[:, :, halves[half]], half_tile("x2g_1%d" % half)))
             for u in range(2):
                 bank = banks[4 + 2 * half + u][:].rearrange("p (t j) -> p t j", t=2)
                 nc.scalar.copy(e1[:, 2 * u : 2 * u + 2, halves[half]], bank)
-        for half in range(2):
-            stage2(0, half, 1, quantise(x2g[half], "x2q_1%d" % half), halves[0])
 
         out_v = out.rearrange("(t p) j -> p t j", p=P)
         for half in range(2):
@@ -274,9 +275,7 @@ def tile_list_pitch_proposal_scores_kernel(
             for u in range(2):
                 bank = banks[2 * half + u][:].rearrange("p (t j) -> p t j", t=2)
                 nc.vector.tensor_tensor(e1[:, 2 * u : 2 * u + 2, js], bank, e1[:, 2 * u : 2 * u + 2, js], ALU.max)
-        for half in range(2):
-            js = halves[half]
-            adder = nc.gpsimd if half == 0 else nc.vector
+            adder = nc.vector
             for u in range(2):
                 res = keep.tile([P, 2, HALF], F32, name="res%d%d" % (half, u))
                 adder.tensor_tensor(res[:], e1[:, 2 * u : 2 * u + 2, js], occ_t[:, 2 * u : 2 * u + 2, js], ALU.add)

@@ -21,6 +21,7 @@ PACK = 4
 PASS = P * PACK
 BANK = 512
 HALF = NP // 2
+FUSED_FROM = 2
 
 
 def tile_list_pitch_proposal_scores_kernel(
@@ -99,9 +100,8 @@ def tile_list_pitch_proposal_scores_kernel(
         occ_t = ring.tile([P, 4, NP], F32, name="occ_t", tag="table", bufs=3)
         nc.sync.dma_start(occ_t[:], occ.rearrange("(t p) j -> p t j", p=P))
 
-        tent_wide = [keep.tile([P, PACK, w], F32, name="tent_wide%d" % b) for b, w in enumerate((NP, NP))]
-        for b in range(2):
-            nc.scalar.copy(tent_wide[b][:], tent_t[:, b, :].unsqueeze(2).to_broadcast(list(tent_wide[b].shape)))
+        tent_wide = keep.tile([P, PACK - FUSED_FROM, NP], F32, name="tent_wide")
+        nc.scalar.copy(tent_wide[:], tent_t[:, 1, FUSED_FROM:].unsqueeze(2).to_broadcast(list(tent_wide.shape)))
 
         v_w = [keep.tile([P, S], U32, name="v_w%d" % a, align_bytes=64) for a in range(3)]
         v_sc = keep.tile([P, S], U8, name="v_sc", align_bytes=64)
@@ -183,15 +183,21 @@ def tile_list_pitch_proposal_scores_kernel(
                     nc.scalar.activation(h[:, js], h[:, js], ACT.Copy, scale=gain_t[:, b, i : i + 1])
             if not first:
                 nc.scalar.activation(h[:], h[:], ACT.Copy, scale=gain_t[:, b, i : i + 1])
-            picks = [
-                (x2, pos2_t, tent_wide[b], ALU.mult),
-                (x1, pos1_t, wish_t[b], ALU.add),
-            ]
             width = HALF if (b, i) == (1, PACK - 1) else NP
             for c in range(0, NP, width):
-                for x, pos, other, op in picks if b == 0 else reversed(picks):
-                    entries = pos[:, c // 16 : (c + width) // 16]
-                    nc.vector.tensor_tensor(x[:, i, c : c + width], h[:].indirect(entries), other[:, i, c : c + width], op)
+                js = slice(c, c + width)
+                entries = slice(c // 16, (c + width) // 16)
+                if b == 0:
+                    nc.vector.tensor_copy(x2[:, i, js], h[:].indirect(pos2_t[:, entries]))
+                nc.vector.tensor_tensor(x1[:, i, js], h[:].indirect(pos1_t[:, entries]), wish_t[b][:, i, js], ALU.add)
+                if b == 1 and i < FUSED_FROM:
+                    nc.vector.tensor_copy(x2[:, i, js], h[:].indirect(pos2_t[:, entries]))
+                elif b == 1:
+                    nc.vector.tensor_tensor(x2[:, i, js], h[:].indirect(pos2_t[:, entries]), tent_wide[:, i - FUSED_FROM, js], ALU.mult)
+
+        def times_tent(x2, b, planes):
+            for i in planes:
+                nc.scalar.activation(x2[:, i, :], x2[:, i, :], ACT.Copy, scale=tent_t[:, b, i : i + 1])
 
         c_w = [keep.tile([P, S2], U32, name="c_w%d" % a, align_bytes=64) for a in range(2)]
         c_sc = keep.tile([P, S2], U8, name="c_sc", align_bytes=64)
@@ -230,10 +236,12 @@ def tile_list_pitch_proposal_scores_kernel(
         x1_1 = picked("x1_1")
         x2_1 = picked("x2_1")
         features(banks1, 1, 0, x1_1, x2_1)
+        times_tent(x2_0, 0, range(PACK))
         x2q_0 = quantise(weave(nc.scalar.copy, x2_0[:], bf_tile(PACK * NP, "x2g_0")), "x2q_0")
         for i in range(1, PACK):
             features(banks1, 1, i, x1_1, x2_1)
         x1q_0 = quantise(weave(nc.scalar.copy, x1_0[:], bf_tile(PACK * NP, "x1g_0")), "x1q_0")
+        times_tent(x2_1, 1, range(FUSED_FROM))
 
         banks = new_banks("e_")
 

@@ -21,7 +21,6 @@ PACK = 4
 PASS = P * PACK
 BANK = 512
 HALF = NP // 2
-FUSED_FROM = 2
 
 
 def tile_list_pitch_proposal_scores_kernel(
@@ -46,12 +45,12 @@ def tile_list_pitch_proposal_scores_kernel(
         for t in (tab_sc, w4_sc_raw, tab2_sc):
             nc.vector.memset(t[:].bitcast(I32), 0)
 
-        freq_t = keep.tile([P, 2, PACK], F32, name="freq_t")
-        gain_t = keep.tile([P, 2, PACK], F32, name="gain_t")
-        tent_t = keep.tile([P, 2, PACK], F32, name="tent_t")
+        freq_t = keep.tile([P, 2, 2 * PACK], F32, name="freq_t")
+        gain_t = keep.tile([P, 2, 2 * PACK], F32, name="gain_t")
+        tent_t = keep.tile([P, 2, 2 * PACK], F32, name="tent_t")
 
-        def load_words(words, a, width, name):
-            t = ring.tile([P, width], I32, name=name, tag="table", bufs=3)
+        def load_words(words, a, width, name, tag):
+            t = ring.tile([P, width], I32, name=name, tag=tag, align_bytes=64)
             nc.sync.dma_start(t[:], words[a].rearrange("p t i -> p (t i)").bitcast(I32))
             return t
 
@@ -66,47 +65,46 @@ def tile_list_pitch_proposal_scores_kernel(
             nc.sync.dma_start(t[:], wish[PASS * b : PASS * (b + 1), :].rearrange("(p i) j -> p i j", i=PACK))
             return t
 
-        def load_rows(t, vec):
-            nc.sync.dma_start(t[:], vec.rearrange("(b p i) -> p b i", b=2, i=PACK))
+        def load_rows(queue, t, vec):
+            queue.dma_start(t[:, :, 0:PACK], vec.rearrange("(b p i) -> p b i", b=2, i=PACK))
 
-        def load_scales(t, scales):
+        def load_scales(queue, t, scales):
             rows = 4 * scales.shape[0]
             for q in range(4):
-                nc.gpsimd.dma_start(t[32 * q : 32 * q + rows, :].bitcast(I32), scales[:, 4 * q : 4 * q + 4, :].bitcast(I32))
+                queue.dma_start(t[32 * q : 32 * q + rows, :].bitcast(I32), scales[:, 4 * q : 4 * q + 4, :].bitcast(I32))
 
-        load_scales(tab_sc, tab_scales)
-        load_scales(w4_sc_raw, w4_scales)
-        load_scales(tab2_sc, tab2_scales)
+        load_rows(nc.gpsimd, tent_t, tent)
+        load_scales(nc.gpsimd, tab_sc, tab_scales)
+        load_scales(nc.gpsimd, tab2_sc, tab2_scales)
         nc.sync.dma_start(offs_t[:], offs)
-        tab_w = [load_words(tab_words, 0, T, "tab0")]
-        load_rows(tent_t, tent)
+        tab_w = [load_words(tab_words, 0, T, "tab0", "table0")]
+        load_scales(nc.sync, w4_sc_raw, w4_scales)
         w4_raw = keep.tile([P, H // 2], I32, name="w4_raw")
         nc.sync.dma_start(w4_raw[:], w4_words[0].bitcast(I32))
-        tab_w.append(load_words(tab_words, 1, T, "tab1"))
-        nc.sync.dma_start(offs2_t[:], offs2)
+        tab_w.append(load_words(tab_words, 1, T, "tab1", "table1"))
         w1_00 = load_w1(0, 0, PASS, "w1_00", "slot_a")
-        tab_w.append(load_words(tab_words, 2, T, "tab2nd"))
-        load_rows(freq_t, freq)
-        load_rows(gain_t, gain)
-        nc.sync.dma_start(pos2_t[:], pos2)
-        nc.sync.dma_start(pos1_t[:], pos1)
+        nc.sync.dma_start(offs2_t[:], offs2)
+        tab_w.append(load_words(tab_words, 2, T, "tab2nd", "table2"))
         w1_10 = [load_w1(1, 0, PASS // 2, "w1_10a", "w1_10a"), load_w1(1, PASS // 2, PASS // 2, "w1_10b", "w1_10b")]
+        load_rows(nc.sync, freq_t, freq)
+        load_rows(nc.sync, gain_t, gain)
+        nc.sync.dma_start(pos2_t[:], pos2)
         w1_01 = load_w1(0, PASS, PASS, "w1_01", "slot_b")
+        nc.sync.dma_start(pos1_t[:], pos1)
         wish_t = [load_wish(0)]
         w1_11 = load_w1(1, PASS, PASS, "w1_11", "w1_11")
-        tab2_w = [load_words(tab2_words, 0, T3, "cand0")]
+        tab2_w = [load_words(tab2_words, 0, T3, "cand0", "table0")]
         wish_t.append(load_wish(1))
-        tab2_w.append(load_words(tab2_words, 1, T3, "cand1"))
-        occ_t = ring.tile([P, 4, NP], F32, name="occ_t", tag="table", bufs=3)
+        tab2_w.append(load_words(tab2_words, 1, T3, "cand1", "table2"))
+        occ_t = ring.tile([P, 4, NP], F32, name="occ_t", tag="w1_11")
         nc.sync.dma_start(occ_t[:], occ.rearrange("(t p) j -> p t j", p=P))
 
-        tent_wide = keep.tile([P, PACK - FUSED_FROM, NP], F32, name="tent_wide")
-        nc.scalar.copy(tent_wide[:], tent_t[:, 1, FUSED_FROM:].unsqueeze(2).to_broadcast(list(tent_wide.shape)))
+        tent_wide = [keep.tile([P, PACK, w], F32, name="tent_wide%d" % b) for b, w in enumerate((NP, NP))]
+        for b in range(2):
+            nc.scalar.copy(tent_wide[b][:], tent_t[:, b, 0:PACK].unsqueeze(2).to_broadcast(list(tent_wide[b].shape)))
 
         v_w = [keep.tile([P, S], U32, name="v_w%d" % a, align_bytes=64) for a in range(3)]
-        v_sc = keep.tile([P, S], U8, name="v_sc", align_bytes=64)
         nc.vector.tensor_copy(v_w[0][:], tab_w[0][:].bitcast(U32).indirect(offs_t[:]))
-        nc.vector.tensor_copy(v_sc[:], tab_sc[:].indirect(offs_t[:]))
 
         w4_c = keep.tile([P, 2 * H], U8, name="w4_c", align_bytes=64)
         w4_sc = keep.tile([P, H], U8, name="w4_sc", align_bytes=64)
@@ -120,6 +118,8 @@ def tile_list_pitch_proposal_scores_kernel(
         )
 
         nc.vector.tensor_copy(v_w[1][:], tab_w[1][:].bitcast(U32).indirect(offs_t[:]))
+        v_sc = ring.tile([P, S], U8, name="v_sc", tag="table1", align_bytes=64)
+        nc.vector.tensor_copy(v_sc[:], tab_sc[:].indirect(offs_t[:]))
 
         def bf_tile(width, name):
             return ring.tile([P, width], BF16, name=name, tag="rounded", bufs=3, align_bytes=64)
@@ -183,31 +183,25 @@ def tile_list_pitch_proposal_scores_kernel(
                     nc.scalar.activation(h[:, js], h[:, js], ACT.Copy, scale=gain_t[:, b, i : i + 1])
             if not first:
                 nc.scalar.activation(h[:], h[:], ACT.Copy, scale=gain_t[:, b, i : i + 1])
+            picks = [
+                (x2, pos2_t, tent_wide[b], ALU.mult),
+                (x1, pos1_t, wish_t[b], ALU.add),
+            ]
             width = HALF if (b, i) == (1, PACK - 1) else NP
             for c in range(0, NP, width):
-                js = slice(c, c + width)
-                entries = slice(c // 16, (c + width) // 16)
-                if b == 0:
-                    nc.vector.tensor_copy(x2[:, i, js], h[:].indirect(pos2_t[:, entries]))
-                nc.vector.tensor_tensor(x1[:, i, js], h[:].indirect(pos1_t[:, entries]), wish_t[b][:, i, js], ALU.add)
-                if b == 1 and i < FUSED_FROM:
-                    nc.vector.tensor_copy(x2[:, i, js], h[:].indirect(pos2_t[:, entries]))
-                elif b == 1:
-                    nc.vector.tensor_tensor(x2[:, i, js], h[:].indirect(pos2_t[:, entries]), tent_wide[:, i - FUSED_FROM, js], ALU.mult)
-
-        def times_tent(x2, b, planes):
-            for i in planes:
-                nc.scalar.activation(x2[:, i, :], x2[:, i, :], ACT.Copy, scale=tent_t[:, b, i : i + 1])
+                for x, pos, other, op in picks if b == 0 else reversed(picks):
+                    entries = pos[:, c // 16 : (c + width) // 16]
+                    nc.vector.tensor_tensor(x[:, i, c : c + width], h[:].indirect(entries), other[:, i, c : c + width], op)
 
         c_w = [keep.tile([P, S2], U32, name="c_w%d" % a, align_bytes=64) for a in range(2)]
-        c_sc = keep.tile([P, S2], U8, name="c_sc", align_bytes=64)
-        nc.vector.tensor_copy(c_sc[:], tab2_sc[:].indirect(offs2_t[:]))
 
         banks0 = new_banks("d0_")
         stage1_pass(banks0, 0, 0, None)
-        g = bf_tile(PACK * PASS, "w1g_00")
+        g = ring.tile([P, PACK * PASS], BF16, name="w1g_00", tag="first_rounded", align_bytes=64)
         deal_w1(nc.scalar.copy, g, w1_00, 0)
         stage1_pass(banks0, 0, 1, quantise(g, "w1q_00"))
+        c_sc = ring.tile([P, S2], U8, name="c_sc", tag="first_rounded", align_bytes=64)
+        nc.vector.tensor_copy(c_sc[:], tab2_sc[:].indirect(offs2_t[:]))
         nc.vector.tensor_copy(v_w[2][:], tab_w[2][:].bitcast(U32).indirect(offs_t[:]))
         g = bf_tile(PACK * PASS, "w1g_10")
         deal_w1(nc.scalar.copy, g, w1_10[0], 0)
@@ -236,12 +230,10 @@ def tile_list_pitch_proposal_scores_kernel(
         x1_1 = picked("x1_1")
         x2_1 = picked("x2_1")
         features(banks1, 1, 0, x1_1, x2_1)
-        times_tent(x2_0, 0, range(PACK))
         x2q_0 = quantise(weave(nc.scalar.copy, x2_0[:], bf_tile(PACK * NP, "x2g_0")), "x2q_0")
         for i in range(1, PACK):
             features(banks1, 1, i, x1_1, x2_1)
         x1q_0 = quantise(weave(nc.scalar.copy, x1_0[:], bf_tile(PACK * NP, "x1g_0")), "x1q_0")
-        times_tent(x2_1, 1, range(FUSED_FROM))
 
         banks = new_banks("e_")
 

from contextlib import ExitStack

import concourse.mybir as mybir

K, K1, T, S, H, T3, S2, NP = 1536, 512, 4096, 1024, 1024, 2048, 512, 512
FLOPS = 2 * K * H * S + 2 * 2 * H * S2 * NP

F32 = mybir.dt.float32
BF16 = mybir.dt.bfloat16
I32 = mybir.dt.int32
U32 = mybir.dt.uint32
U16 = mybir.dt.uint16
U8 = mybir.dt.uint8
FP8X4 = mybir.dt.float8_e4m3fn_x4
FP4X4 = mybir.dt.float4_e2m1fn_x4
ACT = mybir.ActivationFunctionType
ALU = mybir.AluOpType

P = 128
PACK = 4
PASS = P * PACK
BANK = 512
HALF = NP // 2


def tile_list_pitch_proposal_scores_kernel(
    tc, tab_words, tab_scales, offs, tab2_words, tab2_scales, offs2, pos1, pos2,
    w4_words, w4_scales, w1, freq, gain, wish, tent, occ, out,
):
    nc = tc.nc
    with ExitStack() as ctx:
        lists = ctx.enter_context(tc.tile_pool(name="lists", bufs=1))
        keep = ctx.enter_context(tc.tile_pool(name="keep", bufs=1))
        ring = ctx.enter_context(tc.tile_pool(name="ring", bufs=1))
        psum = ctx.enter_context(tc.psum_pool(name="psum", bufs=1))

        offs_t = lists.tile([P, S // 16], U16, name="offs_t")
        offs2_t = lists.tile([P, S2 // 16], U16, name="offs2_t")
        pos1_t = lists.tile([P, NP // 16], U16, name="pos1_t")
        pos2_t = lists.tile([P, NP // 16], U16, name="pos2_t")

        tab_sc = keep.tile([P, T], U8, name="tab_sc")
        w4_sc_raw = keep.tile([P, H], U8, name="w4_sc_raw")
        tab2_sc = keep.tile([P, T3], U8, name="tab2_sc")
        for t in (tab_sc, w4_sc_raw, tab2_sc):
            nc.vector.memset(t[:].bitcast(I32), 0)

        freq_t = keep.tile([P, 2, 2 * PACK], F32, name="freq_t")
        gain_t = keep.tile([P, 2, 2 * PACK], F32, name="gain_t")
        tent_t = keep.tile([P, 2, 2 * PACK], F32, name="tent_t")

        def load_words(words, a, width, name, tag):
            t = ring.tile([P, width], I32, name=name, tag=tag, align_bytes=64)
            nc.sync.dma_start(t[:], words[a].rearrange("p t i -> p (t i)").bitcast(I32))
            return t

        def load_w1(a, c0, width, name, tag):
            t = ring.tile([P, PACK, width], F32, name=name, tag=tag)
            rows = w1[PASS * a : PASS * (a + 1), c0 : c0 + width]
            nc.sync.dma_start(t[:], rows.rearrange("(p j) c -> p j c", j=PACK))
            return t

        def load_wish(b):
            t = keep.tile([P, PACK, NP], F32, name="wish%d" % b)
            nc.sync.dma_start(t[:], wish[PASS * b : PASS * (b + 1), :].rearrange("(p i) j -> p i j", i=PACK))
            return t

        def load_rows(queue, t, vec):
            queue.dma_start(t[:, :, 0:PACK], vec.rearrange("(b p i) -> p b i", b=2, i=PACK))

        def load_scales(queue, t, scales):
            rows = 4 * scales.shape[0]
            for q in range(4):
                queue.dma_start(t[32 * q : 32 * q + rows, :].bitcast(I32), scales[:, 4 * q : 4 * q + 4, :].bitcast(I32))

        load_rows(nc.gpsimd, tent_t, tent)
        load_scales(nc.gpsimd, tab_sc, tab_scales)
        load_scales(nc.gpsimd, tab2_sc, tab2_scales)
        nc.sync.dma_start(offs_t[:], offs)
        tab_w = [load_words(tab_words, 0, T, "tab0", "table0")]
        load_scales(nc.sync, w4_sc_raw, w4_scales)
        w4_raw = keep.tile([P, H // 2], I32, name="w4_raw")
        nc.sync.dma_start(w4_raw[:], w4_words[0].bitcast(I32))
        tab_w.append(load_words(tab_words, 1, T, "tab1", "table1"))
        w1_00 = load_w1(0, 0, PASS, "w1_00", "slot_a")
        nc.sync.dma_start(offs2_t[:], offs2)
        tab_w.append(load_words(tab_words, 2, T, "tab2nd", "table2"))
        w1_10 = [load_w1(1, 0, PASS // 2, "w1_10a", "w1_10a"), load_w1(1, PASS // 2, PASS // 2, "w1_10b", "w1_10b")]
        load_rows(nc.sync, freq_t, freq)
        load_rows(nc.sync, gain_t, gain)
        nc.sync.dma_start(pos2_t[:], pos2)
        w1_01 = load_w1(0, PASS, PASS, "w1_01", "slot_b")
        nc.sync.dma_start(pos1_t[:], pos1)
        wish_t = [load_wish(0)]
        w1_11 = load_w1(1, PASS, PASS, "w1_11", "w1_11")
        tab2_w = [load_words(tab2_words, 0, T3, "cand0", "table0")]
        wish_t.append(load_wish(1))
        tab2_w.append(load_words(tab2_words, 1, T3, "cand1", "table2"))
        occ_t = ring.tile([P, 4, NP], F32, name="occ_t", tag="w1_11")
        nc.sync.dma_start(occ_t[:], occ.rearrange("(t p) j -> p t j", p=P))

        tent_wide = [keep.tile([P, PACK, w], F32, name="tent_wide%d" % b) for b, w in enumerate((NP, NP))]
        for b in range(2):
            nc.scalar.copy(tent_wide[b][:], tent_t[:, b, 0:PACK].unsqueeze(2).to_broadcast(list(tent_wide[b].shape)))

        v_w = [keep.tile([P, S], U32, name="v_w%d" % a, align_bytes=64) for a in range(3)]
        nc.vector.tensor_copy(v_w[0][:], tab_w[0][:].bitcast(U32).indirect(offs_t[:]))

        w4_c = keep.tile([P, 2 * H], U8, name="w4_c", align_bytes=64)
        w4_sc = keep.tile([P, H], U8, name="w4_sc", align_bytes=64)
        nc.vector.tensor_copy(
            w4_c[:].bitcast(U16).rearrange("p (b i q) -> p b i q", b=2, i=PACK),
            w4_raw[:].bitcast(U16).rearrange("p (b q i) -> p b i q", b=2, i=PACK),
        )
        nc.vector.tensor_copy(
            w4_sc[:].rearrange("p (b i q) -> p b i q", b=2, i=PACK),
            w4_sc_raw[:].rearrange("p (b q i) -> p b i q", b=2, i=PACK),
        )

        nc.vector.tensor_copy(v_w[1][:], tab_w[1][:].bitcast(U32).indirect(offs_t[:]))
        v_sc = ring.tile([P, S], U8, name="v_sc", tag="table1", align_bytes=64)
        nc.vector.tensor_copy(v_sc[:], tab_sc[:].indirect(offs_t[:]))

        def bf_tile(width, name):
            return ring.tile([P, width], BF16, name=name, tag="rounded", bufs=3, align_bytes=64)

        def deal_w1(copy, grouped, raw, q0):
            nq = raw.shape[2] // PACK
            dst = grouped[:].rearrange("p (i q j) -> p q j i", i=PACK, j=PACK)[:, q0 : q0 + nq]
            copy(dst, raw[:].rearrange("p j (q i) -> p q j i", i=PACK))

        def quantise(grouped, name, pieces=1):
            width = grouped.shape[1] // PACK
            codes = keep.tile([P, width], U32, name=name + "_c", align_bytes=64)
            scales = keep.tile([P, width], U8, name=name + "_s", align_bytes=64)
            step = width // pieces
            for c in range(0, width, step):
                nc.vector.quantize_mx(
                    out=codes[:, c : c + step].bitcast(FP8X4),
                    scales=scales[:, c : c + step],
                    in_=grouped[:, PACK * c : PACK * (c + step)],
                )
            return codes, scales

        def stage1_pass(banks, b, a, wq):
            for i in range(PACK):
                cols = slice(P * i, P * (i + 1))
                if a == 0:
                    c0 = PASS * b + P * i
                    lhs = w4_c[:, 2 * c0 : 2 * (c0 + P)].bitcast(FP4X4)
                    lhs_sc = w4_sc[:, c0 : c0 + P]
                else:
                    lhs = wq[0][:, cols].bitcast(FP8X4)
                    lhs_sc = wq[1][:, cols]
                for half in range(2):
                    js = slice(BANK * half, BANK * (half + 1))
                    nc.tensor.matmul_mx(
                        out=banks[2 * i + half][:], lhsT=lhs, lhsT_scale=lhs_sc,
                        rhs=v_w[a][:, js].bitcast(FP8X4), rhs_scale=v_sc[4 * a :, js],
                        start=(a == 0), stop=(a == 2),
                    )

        def new_banks(name):
            return [psum.tile([P, BANK], F32, name="%s%d" % (name, k), tag="bank%d" % k) for k in range(8)]

        def picked(name, tag="picked", bufs=3):
            return ring.tile([P, PACK, NP], F32, name=name, tag=tag, bufs=bufs)

        def weave(copy, src, dst):
            copy(
                dst[:].rearrange("p (c k i) -> p c i k", k=4, i=PACK),
                src.rearrange("p i (c k) -> p c i k", k=4),
            )
            return dst

        def features(banks, b, i, x1, x2):
            h = ring.tile([P, S], F32, name="h%d%d" % (b, i), tag="h", bufs=4)
            first = (b, i) == (0, 0)
            for half in range(2):
                js = slice(BANK * half, BANK * (half + 1))
                nc.scalar.activation(h[:, js], banks[2 * i + half][:], ACT.Sin, scale=freq_t[:, b, i : i + 1])
                if first:
                    nc.scalar.activation(h[:, js], h[:, js], ACT.Copy, scale=gain_t[:, b, i : i + 1])
            if not first:
                nc.scalar.activation(h[:], h[:], ACT.Copy, scale=gain_t[:, b, i : i + 1])
            picks = [
                (x2, pos2_t, tent_wide[b], ALU.mult),
                (x1, pos1_t, wish_t[b], ALU.add),
            ]
            width = HALF if (b, i) == (1, PACK - 1) else NP
            for c in range(0, NP, width):
                for x, pos, other, op in picks if b == 0 else reversed(picks):
                    entries = pos[:, c // 16 : (c + width) // 16]
                    nc.vector.tensor_tensor(x[:, i, c : c + width], h[:].indirect(entries), other[:, i, c : c + width], op)

        c_w = [keep.tile([P, S2], U32, name="c_w%d" % a, align_bytes=64) for a in range(2)]

        banks0 = new_banks("d0_")
        stage1_pass(banks0, 0, 0, None)
        g = ring.tile([P, PACK * PASS], BF16, name="w1g_00", tag="first_rounded", align_bytes=64)
        deal_w1(nc.scalar.copy, g, w1_00, 0)
        stage1_pass(banks0, 0, 1, quantise(g, "w1q_00"))
        c_sc = ring.tile([P, S2], U8, name="c_sc", tag="first_rounded", align_bytes=64)
        nc.vector.tensor_copy(c_sc[:], tab2_sc[:].indirect(offs2_t[:]))
        nc.vector.tensor_copy(v_w[2][:], tab_w[2][:].bitcast(U32).indirect(offs_t[:]))
        g = bf_tile(PACK * PASS, "w1g_10")
        deal_w1(nc.scalar.copy, g, w1_10[0], 0)
        deal_w1(nc.vector.tensor_copy, g, w1_10[1], P // 2)
        stage1_pass(banks0, 0, 2, quantise(g, "w1q_10", pieces=PACK))
        g = bf_tile(PACK * PASS, "w1g_01")
        deal_w1(nc.vector.tensor_copy, g, w1_01, 0)
        w1q_01 = quantise(g, "w1q_01")

        x2_0 = picked("x2_0", "slot_a", 1)
        x1_0 = picked("x1_0")
        for i in range(PACK - 1):
            features(banks0, 0, i, x1_0, x2_0)
        g = bf_tile(PACK * PASS, "w1g_11")
        deal_w1(nc.scalar.copy, g, w1_11, 0)
        w1q_11 = quantise(g, "w1q_11")
        features(banks0, 0, PACK - 1, x1_0, x2_0)

        banks1 = new_banks("d1_")
        stage1_pass(banks1, 1, 0, None)
        stage1_pass(banks1, 1, 1, w1q_01)
        stage1_pass(banks1, 1, 2, w1q_11)
        for a in range(2):
            nc.vector.tensor_copy(c_w[a][:], tab2_w[a][:].bitcast(U32).indirect(offs2_t[:]))

        x1_1 = picked("x1_1")
        x2_1 = picked("x2_1")
        features(banks1, 1, 0, x1_1, x2_1)
        x2q_0 = quantise(weave(nc.scalar.copy, x2_0[:], bf_tile(PACK * NP, "x2g_0")), "x2q_0")
        for i in range(1, PACK):
            features(banks1, 1, i, x1_1, x2_1)
        x1q_0 = quantise(weave(nc.scalar.copy, x1_0[:], bf_tile(PACK * NP, "x1g_0")), "x1q_0")

        banks = new_banks("e_")

        def stage2(side, half, b, xq, js):
            for mt in range(4):
                cols = slice(P * mt, P * (mt + 1))
                nc.tensor.matmul_mx(
                    out=banks[4 * side + 2 * half + mt // 2][:, HALF * (mt % 2) : HALF * (mt % 2 + 1)],
                    lhsT=c_w[b][:, cols].bitcast(FP8X4), lhsT_scale=c_sc[4 * b :, cols],
                    rhs=xq[0][:, js].bitcast(FP8X4), rhs_scale=xq[1][:, js],
                    start=(b == 0 and mt % 2 == 0), stop=(b == 1 and mt % 2 == 1),
                )

        halves = [slice(HALF * half, HALF * (half + 1)) for half in range(2)]
        for side, xq in ((0, x2q_0), (1, x1q_0)):
            for half in range(2):
                stage2(side, half, 0, xq, halves[half])

        def half_tile(name):
            return ring.tile([P, PACK * HALF], BF16, name=name, tag="half", bufs=4, align_bytes=64)

        e1 = ring.tile([P, 4, NP], F32, name="e1", tag="slot_b")
        x1g = [weave(nc.scalar.copy, x1_1[:, :, halves[0]], half_tile("x1g_10"))]
        x2g = [weave(nc.scalar.copy, x2_1[:, :, halves[0]], half_tile("x2g_10"))]
        x1g.append(weave(nc.scalar.copy, x1_1[:, :, halves[1]], half_tile("x1g_11")))
        stage2(1, 0, 1, quantise(x1g[0], "x1q_10"), halves[0])
        x2g.append(weave(nc.vector.tensor_copy, x2_1[:, :, halves[1]], half_tile("x2g_11")))
        stage2(0, 0, 1, quantise(x2g[0], "x2q_10"), halves[0])
        stage2(1, 1, 1, quantise(x1g[1], "x1q_11"), halves[0])
        stage2(0, 1, 1, quantise(x2g[1], "x2q_11"), halves[0])
        for half in range(2):
            for u in range(2):
                bank = banks[4 + 2 * half + u][:].rearrange("p (t j) -> p t j", t=2)
                nc.scalar.copy(e1[:, 2 * u : 2 * u + 2, halves[half]], bank)

        out_v = out.rearrange("(t p) j -> p t j", p=P)
        for half in range(2):
            js = halves[half]
            for u in range(2):
                bank = banks[2 * half + u][:].rearrange("p (t j) -> p t j", t=2)
                nc.vector.tensor_tensor(e1[:, 2 * u : 2 * u + 2, js], bank, e1[:, 2 * u : 2 * u + 2, js], ALU.max)
            adder = nc.vector
            for u in range(2):
                res = keep.tile([P, 2, HALF], F32, name="res%d%d" % (half, u))
                adder.tensor_tensor(res[:], e1[:, 2 * u : 2 * u + 2, js], occ_t[:, 2 * u : 2 * u + 2, js], ALU.add)
                nc.sync.dma_start(out_v[:, 2 * u : 2 * u + 2, js], res[:])
